import numpy as np, ml_dtypes
CORES = [2,34,66,98,130,162,194,226,258,290,322,354,386,418,450,482]
N = 16
F = 64
GROUPS = [[0,1,2,5,7,10,12,15],[3,4,6,8,9,11,13,14]]
def setup_inputs(rng):
    return {"x": rng.standard_normal((N, 128, F), dtype=np.float32).astype(ml_dtypes.bfloat16), "w": (rng.standard_normal((N, 128, 128), dtype=np.float32) / 11).astype(ml_dtypes.bfloat16)}
def setup_inputs_big(rng):
    d = setup_inputs(rng)
    for k in ("x", "w"): d[k] = (d[k].astype(np.float32) * 1024.0).astype(d[k].dtype)
    return d
def setup_inputs_small(rng):
    d = setup_inputs(rng)
    for k in ("x", "w"): d[k] = (d[k].astype(np.float32) * (1 / 1024.0)).astype(d[k].dtype)
    return d
def setup_inputs_apart(rng):
    d = setup_inputs(rng)
    f = (10.0 ** rng.permutation(np.linspace(-1.5, 1.5, N))).astype(np.float32).reshape(N, 1, 1)
    for k in ("x", "w"): d[k] = (d[k].astype(np.float32) * f).astype(d[k].dtype)
    return d
def reference(x, w):
    X, W = x.astype(np.float64), w.astype(np.float64)
    s = sum(W[g[0]].T @ np.maximum(sum(X[j] for j in g), 0.0) for g in GROUPS).astype(ml_dtypes.bfloat16)
    return {"y": np.broadcast_to(s, (N,) + s.shape)}

@@ -1,0 +1,184 @@
+from concourse.bass import DstId, RemoteDMATransfer
+from concourse.mybir import AluOpType
+
+F = 64
+M = 128
+PW = 2 * F
+P_OFS = [M, M + PW, 2 * M + 2 * PW, 2 * M + 3 * PW]
+W_OFS = [0, M + 2 * PW]
+SPAN = [(0, M + PW), (M + PW, 2 * M + 2 * PW), (2 * M + 2 * PW, 2 * M + 3 * PW), (2 * M + 3 * PW, 2 * M + 4 * PW)]
+
+SCRATCH = {
+    "big": ("sbuf", [128, 2 * M + 4 * PW], "bfloat16"),
+    "slots": ("sbuf", [128, 3 * PW], "bfloat16"),
+    "zero": ("sbuf", [128, PW], "float32"),
+    "t": ("sbuf", [128, PW], "bfloat16"),
+    "ysb": ("sbuf", [128, F], "bfloat16"),
+    "acc": ("psum", [128, 512], "float32"),
+    "yp": ("psum", [128, 512], "float32"),
+}
+SEMAPHORES = ["ld", "h1", "s1", "s2", "z", "v1", "v2", "a0", "a1", "a2", "a3", "mm", "cp", "st"]
+
+
+def _plan(cores, groups, topo):
+    n = len(cores)
+    grp = {}
+    for gi, mem in enumerate(groups):
+        for r in mem:
+            grp[r] = gi
+    lead = [mem[0] for mem in groups]
+    hosts = sorted(set(topo.host(c) for c in cores))
+    of_host = {}
+    for h in hosts:
+        of_host[h] = sorted((r for r in range(n) if topo.host(cores[r]) == h), key=lambda r: topo.chip(cores[r]))
+    near = [h for h in hosts if topo.rack(h) == topo.rack(hosts[0])]
+    far = [h for h in hosts if topo.rack(h) != topo.rack(hosts[0])]
+    pairs = []
+    for h in near:
+        k = [k for k in far if topo.may_write(cores[of_host[h][0]], cores[of_host[k][0]])]
+        pairs.append((h, k[0]))
+    cols = None
+    for other in (1, 2, 3):
+        halves = [(0, other), tuple(i for i in (1, 2, 3) if i != other)]
+        cand = []
+        for h, k in pairs:
+            for half in halves:
+                cand.append([of_host[h][i] for i in half] + [of_host[k][i] for i in half])
+        where = {}
+        for q, col in enumerate(cand):
+            for r in col:
+                where[r] = q
+        if where[lead[0]] != where[lead[1]]:
+            first = [where[lead[0]], where[lead[1]]]
+            cols = [cand[q] for q in first] + [cand[q] for q in range(len(cand)) if q not in first]
+            break
+    assert cols is not None and len(cols) == 4
+    return cols, grp, lead
+
+
+def _members(col, q, grp, lead):
+    mem = [[r for r in col if grp[r] == gi] for gi in (0, 1)]
+    for gi in (0, 1):
+        if lead[gi] in mem[gi]:
+            mem[gi] = [lead[gi]] + [r for r in mem[gi] if r != lead[gi]]
+    return mem
+
+
+def _mask(topo, src, dests):
+    m = topo.mask(src, dests[0])
+    for d in dests[1:]:
+        m &= topo.mask(src, d)
+    return m
+
+
+def _engines(topo, src, dests):
+    return bin(_mask(topo, src, dests)).count("1")
+
+
+def _send(g, topo, core, dests, ap, remote_sem, local_sem):
+    ids = []
+    for d in dests:
+        rid, pid = topo.addr(d, core)
+        ids.append(DstId(rid=rid, pnc=pid))
+    g.remote_dma_fused([RemoteDMATransfer(dst_ids=ids, dma_engine_mask=_mask(topo, core, dests), remote_sem=remote_sem,
+                                          srcs=[ap], dsts=[ap for _ in dests])], local_sem=local_sem)
+
+
+def rank_program(g, core, T, topo):
+    rank = T.rank_of(core)
+    if rank is None:
+        return
+    cores = T.cores
+    cols, grp, lead = _plan(cores, T.tables["GROUPS"], topo)
+    q = [i for i, c in enumerate(cols) if rank in c][0]
+    col = cols[q]
+    j = col.index(rank)
+    row = [c[j] for c in cols]
+    mem = _members(col, q, grp, lead)
+    sem, v, big = T.sem, g.vector, T.big
+    gi = grp[rank]
+    k = mem[gi].index(rank)
+    po = P_OFS[q]
+
+    def mates(ranks, r):
+        return [cores[o] for o in ranks if o != r]
+
+    if k == 0:
+        xap = big[:, po + gi * F: po + (gi + 1) * F]
+    else:
+        xap = T.slots[:, (k - 1) * PW + gi * F: (k - 1) * PW + (gi + 1) * F]
+    nld = 16
+    if rank == lead[gi]:
+        g.scalar.dma_start(big[:, W_OFS[gi]: W_OFS[gi] + M], T.w[:, :]).then_inc(sem.ld, 16)
+        nld += 16
+    g.sync.dma_start(xap, T.x[:, :]).then_inc(sem.ld, 16)
+    v.memset(T.zero[:, :], 0.0).then_inc(sem.z, 1)
+
+    if rank == lead[0]:
+        out1 = big[:, W_OFS[0]: po + F]
+    elif rank == lead[1]:
+        out1 = big[:, po + F: W_OFS[1] + M]
+    else:
+        out1 = xap
+    g.wait_ge(sem.ld, nld)
+    _send(g, topo, core, mates(col, rank), out1, sem.h1, sem.s1)
+    n1 = sum(_engines(topo, cores[o], mates(col, o)) for o in col if o != rank)
+    e1 = _engines(topo, core, mates(col, rank))
+
+    nv = 0
+    for a in (0, 1):
+        if not mem[a]:
+            v.memset(big[:, po + a * F: po + (a + 1) * F], 0.0).then_inc(sem.v1, 1)
+            nv += 1
+    v.wait_ge(sem.ld, nld)
+    v.wait_ge(sem.h1, n1)
+    if k == 0 and len(mem[gi]) > 1:
+        v.wait_ge(sem.s1, e1)
+    for rnd in range(max(len(mem[0]), len(mem[1])) - 1):
+        act = [a for a in (0, 1) if len(mem[a]) - 1 > rnd]
+        lo, hi = act[0] * F, (act[-1] + 1) * F
+        if nv:
+            v.wait_ge(sem.v1, nv)
+        v.tensor_tensor(out=big[:, po + lo: po + hi], in0=big[:, po + lo: po + hi],
+                        in1=T.slots[:, rnd * PW + lo: rnd * PW + hi], op=AluOpType.add).then_inc(sem.v1, 1)
+        nv += 1
+
+    g.wait_ge(sem.h1, n1)
+    if nv:
+        g.wait_ge(sem.v1, nv)
+    _send(g, topo, core, mates(row, rank), big[:, SPAN[q][0]: SPAN[q][1]], sem["a%d" % q], sem.s2)
+    e2 = _engines(topo, core, mates(row, rank))
+
+    order = [p for p in (2, 3, 0, 1) if p != q]
+    acc = T.acc[:, 0:PW]
+    if nv:
+        v.wait_ge(sem.v1, nv)
+    n2 = 0
+    for p in order:
+        v.wait_ge(sem["a%d" % p], _engines(topo, cores[row[p]], mates(row, row[p])))
+        if n2:
+            v.wait_ge(sem.v2, n2)
+        v.tensor_tensor(out=acc, in0=(acc if n2 else big[:, po: po + PW]), in1=big[:, P_OFS[p]: P_OFS[p] + PW],
+                        op=AluOpType.add).then_inc(sem.v2, 1)
+        n2 += 1
+    v.wait_ge(sem.z, 1)
+    v.wait_ge(sem.v2, n2)
+    v.tensor_tensor(out=T.t[:, :], in0=acc, in1=T.zero[:, :], op=AluOpType.max).then_inc(sem.v2, 1)
+    n2 += 1
+
+    te = g.tensor
+    te.wait_ge(sem.ld, nld)
+    te.wait_ge(sem.h1, n1)
+    for p in order:
+        te.wait_ge(sem["a%d" % p], _engines(topo, cores[row[p]], mates(row, row[p])))
+    te.wait_ge(sem.v2, n2)
+    te.matmul(T.yp[:, 0:F], big[:, W_OFS[0]: W_OFS[0] + M], T.t[:, 0:F], True, False)
+    te.matmul(T.yp[:, 0:F], big[:, W_OFS[1]: W_OFS[1] + M], T.t[:, F:PW], False, True).then_inc(sem.mm, 1)
+    v.wait_ge(sem.mm, 1)
+    v.tensor_copy(T.ysb[:, :], T.yp[:, 0:F]).then_inc(sem.cp, 1)
+    g.sync.wait_ge(sem.cp, 1)
+    g.sync.dma_start(T.y[:, :], T.ysb[:, :]).then_inc(sem.st, 16)
+
+    g.wait_ge(sem.s1, e1)
+    g.wait_ge(sem.s2, e2)
+    g.wait_ge(sem.st, 16)

@@ -3,182 +3,186 @@ from concourse.mybir import AluOpType
 
 F = 64
 M = 128
-PW = 2 * F
-P_OFS = [M, M + PW, 2 * M + 2 * PW, 2 * M + 3 * PW]
-W_OFS = [0, M + 2 * PW]
-SPAN = [(0, M + PW), (M + PW, 2 * M + 2 * PW), (2 * M + 2 * PW, 2 * M + 3 * PW), (2 * M + 3 * PW, 2 * M + 4 * PW)]
+HALF = 8
+Q = 4
+FQ = F // Q
 
 SCRATCH = {
-    "big": ("sbuf", [128, 2 * M + 4 * PW], "bfloat16"),
-    "slots": ("sbuf", [128, 3 * PW], "bfloat16"),
-    "zero": ("sbuf", [128, PW], "float32"),
-    "t": ("sbuf", [128, PW], "bfloat16"),
+    "xq": ("dram", [Q, 128, FQ], "bfloat16"),
+    "xs": ("dram", [HALF, 128, FQ], "bfloat16"),
+    "pd": ("dram", [4 * Q, 128, FQ], "bfloat16"),
+    "wd": ("dram", [2, 128, M], "bfloat16"),
+    "z": ("sbuf", [128, 4 * F], "bfloat16"),
+    "ww": ("sbuf", [128, 2 * M], "bfloat16"),
+    "tb": ("sbuf", [128, 2 * F], "bfloat16"),
+    "t": ("sbuf", [128, 2 * F], "bfloat16"),
     "ysb": ("sbuf", [128, F], "bfloat16"),
-    "acc": ("psum", [128, 512], "float32"),
     "yp": ("psum", [128, 512], "float32"),
 }
-SEMAPHORES = ["ld", "h1", "s1", "s2", "z", "v1", "v2", "a0", "a1", "a2", "a3", "mm", "cp", "st"]
+SEMAPHORES = ["ld", "lw", "hx", "w0", "w1", "p", "s", "lz", "lww", "v", "mm", "cp", "st"]
 
 
 def _plan(cores, groups, topo):
     n = len(cores)
-    grp = {}
-    for gi, mem in enumerate(groups):
-        for r in mem:
-            grp[r] = gi
     lead = [mem[0] for mem in groups]
-    hosts = sorted(set(topo.host(c) for c in cores))
-    of_host = {}
-    for h in hosts:
-        of_host[h] = sorted((r for r in range(n) if topo.host(cores[r]) == h), key=lambda r: topo.chip(cores[r]))
-    near = [h for h in hosts if topo.rack(h) == topo.rack(hosts[0])]
-    far = [h for h in hosts if topo.rack(h) != topo.rack(hosts[0])]
-    pairs = []
-    for h in near:
-        k = [k for k in far if topo.may_write(cores[of_host[h][0]], cores[of_host[k][0]])]
-        pairs.append((h, k[0]))
-    cols = None
-    for other in (1, 2, 3):
-        halves = [(0, other), tuple(i for i in (1, 2, 3) if i != other)]
-        cand = []
-        for h, k in pairs:
-            for half in halves:
-                cand.append([of_host[h][i] for i in half] + [of_host[k][i] for i in half])
-        where = {}
-        for q, col in enumerate(cand):
-            for r in col:
-                where[r] = q
-        if where[lead[0]] != where[lead[1]]:
-            first = [where[lead[0]], where[lead[1]]]
-            cols = [cand[q] for q in first] + [cand[q] for q in range(len(cand)) if q not in first]
-            break
-    assert cols is not None and len(cols) == 4
-    return cols, grp, lead
+    hs = [topo.host(c) for c in cores]
+    rk = [topo.rack(h) for h in hs]
+    hm, mem = {}, {}
+    for r in sorted(range(n), key=lambda r: topo.chip(cores[r])):
+        hm.setdefault(hs[r], []).append(r)
+    for r in range(n):
+        mem.setdefault(rk[r], []).append(r)
+    pos = [hm[hs[r]].index(r) for r in range(n)]
+
+    def ok(a, b):
+        return topo.may_write(cores[a], cores[b])
+
+    def off(a, b):
+        return topo.chip(cores[a]) != topo.chip(cores[b])
+
+    xdst = [[[d for d in mem[rk[r]] if pos[d] == k and d != r] for k in range(Q)] for r in range(n)]
+    pdst = [[d for d in range(n) if d != r and ((rk[d] == rk[r] and (hs[d] == hs[r] or pos[d] == pos[r]))
+                                                or (rk[d] != rk[r] and ok(r, d)))] for r in range(n)]
+    duty = [0] * n
+    w1, w2 = [], []
+    for o in lead:
+        near = [r for r in mem[rk[o]] if hs[r] != hs[o]]
+        far = [r for r in range(n) if rk[r] != rk[o] and ok(o, r)]
+        diag = [r for r in range(n) if rk[r] != rk[o] and not ok(o, r)]
+        b = min(far, key=lambda r: (duty[r], off(r, o), r))
+        a = sorted(near, key=lambda r: (duty[r], off(r, o), r))[:2]
+        for r in a + [b]:
+            duty[r] += 1
+        out = {o: [r for r in hm[hs[o]] if r != o], b: [r for r in far if r != b]}
+        for r in a:
+            out[r] = []
+        for d in [r for r in near if r not in a] + diag:
+            s = min([s for s in a if ok(s, d)], key=lambda s: (len(out[s]), off(s, d), s))
+            out[s].append(d)
+        w1.append(a + [b])
+        w2.append(out)
+    return lead, rk, mem, pos, xdst, pdst, w1, w2
 
 
-def _members(col, q, grp, lead):
-    mem = [[r for r in col if grp[r] == gi] for gi in (0, 1)]
-    for gi in (0, 1):
-        if lead[gi] in mem[gi]:
-            mem[gi] = [lead[gi]] + [r for r in mem[gi] if r != lead[gi]]
-    return mem
-
-
-def _mask(topo, src, dests):
+def _bits(topo, src, dests):
     m = topo.mask(src, dests[0])
     for d in dests[1:]:
         m &= topo.mask(src, d)
-    return m
+    return [i for i in range(16) if (m >> i) & 1]
 
 
-def _engines(topo, src, dests):
-    return bin(_mask(topo, src, dests)).count("1")
+def _m(bits):
+    return sum(1 << i for i in bits)
 
 
-def _send(g, topo, core, dests, ap, remote_sem, local_sem):
-    ids = []
+def _ids(topo, core, dests):
+    out = []
     for d in dests:
         rid, pid = topo.addr(d, core)
-        ids.append(DstId(rid=rid, pnc=pid))
-    g.remote_dma_fused([RemoteDMATransfer(dst_ids=ids, dma_engine_mask=_mask(topo, core, dests), remote_sem=remote_sem,
-                                          srcs=[ap], dsts=[ap for _ in dests])], local_sem=local_sem)
+        out.append(DstId(rid=rid, pnc=pid))
+    return out
 
 
 def rank_program(g, core, T, topo):
     rank = T.rank_of(core)
     if rank is None:
         return
-    cores = T.cores
-    cols, grp, lead = _plan(cores, T.tables["GROUPS"], topo)
-    q = [i for i, c in enumerate(cols) if rank in c][0]
-    col = cols[q]
-    j = col.index(rank)
-    row = [c[j] for c in cols]
-    mem = _members(col, q, grp, lead)
-    sem, v, big = T.sem, g.vector, T.big
-    gi = grp[rank]
-    k = mem[gi].index(rank)
-    po = P_OFS[q]
+    cores, groups = T.cores, T.tables["GROUPS"]
+    n = len(cores)
+    lead, rk, mem, pos, xdst, pdst, w1, w2 = _plan(cores, groups, topo)
+    sem, v, te = T.sem, g.vector, g.tensor
+    wsem = [sem.w0, sem.w1]
+    q = rk[rank]
+    mine = mem[q]
+    k = pos[rank]
+    own = [gi for gi in range(2) if lead[gi] == rank]
+    sent = [0]
 
-    def mates(ranks, r):
-        return [cores[o] for o in ranks if o != r]
+    def cs(ranks):
+        return [cores[r] for r in ranks]
 
-    if k == 0:
-        xap = big[:, po + gi * F: po + (gi + 1) * F]
-    else:
-        xap = T.slots[:, (k - 1) * PW + gi * F: (k - 1) * PW + (gi + 1) * F]
-    nld = 16
-    if rank == lead[gi]:
-        g.scalar.dma_start(big[:, W_OFS[gi]: W_OFS[gi] + M], T.w[:, :]).then_inc(sem.ld, 16)
-        nld += 16
-    g.sync.dma_start(xap, T.x[:, :]).then_inc(sem.ld, 16)
-    v.memset(T.zero[:, :], 0.0).then_inc(sem.z, 1)
+    def xbits(r):
+        return _bits(topo, cores[r], cs([d for d in mem[rk[r]] if d != r]))
 
-    if rank == lead[0]:
-        out1 = big[:, W_OFS[0]: po + F]
-    elif rank == lead[1]:
-        out1 = big[:, po + F: W_OFS[1] + M]
-    else:
-        out1 = xap
-    g.wait_ge(sem.ld, nld)
-    _send(g, topo, core, mates(col, rank), out1, sem.h1, sem.s1)
-    n1 = sum(_engines(topo, cores[o], mates(col, o)) for o in col if o != rank)
-    e1 = _engines(topo, core, mates(col, rank))
+    def pbits(r):
+        return _bits(topo, cores[r], cs(pdst[r]))
 
-    nv = 0
-    for a in (0, 1):
-        if not mem[a]:
-            v.memset(big[:, po + a * F: po + (a + 1) * F], 0.0).then_inc(sem.v1, 1)
-            nv += 1
-    v.wait_ge(sem.ld, nld)
-    v.wait_ge(sem.h1, n1)
-    if k == 0 and len(mem[gi]) > 1:
-        v.wait_ge(sem.s1, e1)
-    for rnd in range(max(len(mem[0]), len(mem[1])) - 1):
-        act = [a for a in (0, 1) if len(mem[a]) - 1 > rnd]
-        lo, hi = act[0] * F, (act[-1] + 1) * F
-        if nv:
-            v.wait_ge(sem.v1, nv)
-        v.tensor_tensor(out=big[:, po + lo: po + hi], in0=big[:, po + lo: po + hi],
-                        in1=T.slots[:, rnd * PW + lo: rnd * PW + hi], op=AluOpType.add).then_inc(sem.v1, 1)
-        nv += 1
+    def send_w(gi, to):
+        b = _bits(topo, core, cs(to))
+        g.remote_dma_fused([RemoteDMATransfer(dst_ids=_ids(topo, core, cs(to)), dma_engine_mask=_m(b), remote_sem=wsem[gi],
+                                              srcs=[T.wd[gi]], dsts=[T.wd[gi] for _ in to])], local_sem=sem.s)
+        sent[0] += len(b)
 
-    g.wait_ge(sem.h1, n1)
-    if nv:
-        g.wait_ge(sem.v1, nv)
-    _send(g, topo, core, mates(row, rank), big[:, SPAN[q][0]: SPAN[q][1]], sem["a%d" % q], sem.s2)
-    e2 = _engines(topo, core, mates(row, rank))
+    g.sync.dma_start(T.xq[:], T.x[:, :]).then_inc(sem.ld, 16)
+    for gi in own:
+        g.scalar.dma_start(T.wd[gi], T.w[:, :]).then_inc(sem.lw, 16)
 
-    order = [p for p in (2, 3, 0, 1) if p != q]
-    acc = T.acc[:, 0:PW]
-    if nv:
-        v.wait_ge(sem.v1, nv)
-    n2 = 0
-    for p in order:
-        v.wait_ge(sem["a%d" % p], _engines(topo, cores[row[p]], mates(row, row[p])))
-        if n2:
-            v.wait_ge(sem.v2, n2)
-        v.tensor_tensor(out=acc, in0=(acc if n2 else big[:, po: po + PW]), in1=big[:, P_OFS[p]: P_OFS[p] + PW],
-                        op=AluOpType.add).then_inc(sem.v2, 1)
-        n2 += 1
-    v.wait_ge(sem.z, 1)
-    v.wait_ge(sem.v2, n2)
-    v.tensor_tensor(out=T.t[:, :], in0=acc, in1=T.zero[:, :], op=AluOpType.max).then_inc(sem.v2, 1)
-    n2 += 1
+    b = xbits(rank)
+    e = len(b) // Q
+    trs = []
+    for j in range(Q):
+        to = cs(xdst[rank][j])
+        trs.append(RemoteDMATransfer(dst_ids=_ids(topo, core, to), dma_engine_mask=_m(b[j * e:(j + 1) * e]), remote_sem=sem.hx,
+                                     srcs=[T.xq[j]], dsts=[T.xs[mine.index(rank)] for _ in to]))
+        sent[0] += e
+    g.wait_ge(sem.ld, 16)
+    g.remote_dma_fused(trs, local_sem=sem.s)
 
-    te = g.tensor
-    te.wait_ge(sem.ld, nld)
-    te.wait_ge(sem.h1, n1)
-    for p in order:
-        te.wait_ge(sem["a%d" % p], _engines(topo, cores[row[p]], mates(row, row[p])))
-    te.wait_ge(sem.v2, n2)
-    te.matmul(T.yp[:, 0:F], big[:, W_OFS[0]: W_OFS[0] + M], T.t[:, 0:F], True, False)
-    te.matmul(T.yp[:, 0:F], big[:, W_OFS[1]: W_OFS[1] + M], T.t[:, F:PW], False, True).then_inc(sem.mm, 1)
+    for gi in own:
+        g.wait_ge(sem.lw, 16 * len(own))
+        send_w(gi, w1[gi])
+
+    g.wait_ge(sem.hx, sum(len(xbits(o)) // Q for o in mine if o != rank))
+    b = pbits(rank)
+    h = len(b) // 2
+    trs = []
+    for gi in range(2):
+        srcs = [(T.xq[k] if r == rank else T.xs[mine.index(r)]) for r in groups[gi] if r in mine]
+        assert srcs
+        trs.append(RemoteDMATransfer(dst_ids=_ids(topo, core, cs(pdst[rank])), dma_engine_mask=_m(b[gi * h:(gi + 1) * h]),
+                                     remote_sem=sem.p, srcs=srcs, alu_op=(1 if len(srcs) > 1 else 0),
+                                     dsts=[T.pd[(0 if rk[d] == q else 2 * Q) + gi * Q + k] for d in pdst[rank]]))
+        sent[0] += h
+    g.remote_dma_fused(trs, local_sem=sem.s)
+
+    def w_in(gi):
+        for s in [lead[gi]] + list(w2[gi]):
+            to = w1[gi] if (s == lead[gi] and rank in w1[gi]) else w2[gi][s]
+            if rank in to:
+                return len(_bits(topo, cores[s], cs(to)))
+        return 0
+
+    for gi in own:
+        send_w(gi, w2[gi][rank])
+    for gi in range(2):
+        if gi not in own and rank in w2[gi] and w2[gi][rank]:
+            g.wait_ge(wsem[gi], w_in(gi))
+            send_w(gi, w2[gi][rank])
+
+    npd = sum(2 * (len(pbits(s)) // 2) for s in range(n) if rank in pdst[s])
+    for i, qu in enumerate((g.sync, g.scalar)):
+        qu.wait_ge(sem.p, npd)
+        qu.dma_start(T.z[:, i * 2 * F:(i + 1) * 2 * F], T.pd[i * 2 * Q:(i + 1) * 2 * Q]).then_inc(sem.lz, 16)
+    for gi, qu in enumerate((g.sync, g.scalar)):
+        if gi in own:
+            qu.wait_ge(sem.lw, 16 * len(own))
+        else:
+            qu.wait_ge(wsem[gi], w_in(gi))
+        qu.dma_start(T.ww[gi * 64:(gi + 1) * 64, :], T.wd[gi]).then_inc(sem.lww, 16)
+
+    v.wait_ge(sem.lz, 32)
+    v.tensor_tensor(out=T.tb[:, :], in0=T.z[:, 0:2 * F], in1=T.z[:, 2 * F:4 * F], op=AluOpType.add).then_inc(sem.v, 1)
+    v.wait_ge(sem.v, 1)
+    v.tensor_scalar(out=T.t[:, :], in0=T.tb[:, :], scalar1=0.0, scalar2=None, op0=AluOpType.max).then_inc(sem.v, 1)
+
+    te.wait_ge(sem.lww, 32)
+    te.wait_ge(sem.v, 2)
+    te.matmul(T.yp[:, 0:F], T.ww[:, 0:M], T.t[:, 0:F], True, False)
+    te.matmul(T.yp[:, 0:F], T.ww[:, M:2 * M], T.t[:, F:2 * F], False, True).then_inc(sem.mm, 1)
     v.wait_ge(sem.mm, 1)
     v.tensor_copy(T.ysb[:, :], T.yp[:, 0:F]).then_inc(sem.cp, 1)
     g.sync.wait_ge(sem.cp, 1)
     g.sync.dma_start(T.y[:, :], T.ysb[:, :]).then_inc(sem.st, 16)
 
-    g.wait_ge(sem.s1, e1)
-    g.wait_ge(sem.s2, e2)
+    g.wait_ge(sem.s, sent[0])
     g.wait_ge(sem.st, 16)

@@ -6,12 +6,14 @@ M = 128
 HALF = 8
 Q = 4
 FQ = F // Q
+MQ = M // Q
+EP = 2
 
 SCRATCH = {
     "xq": ("dram", [Q, 128, FQ], "bfloat16"),
     "xs": ("dram", [HALF, 128, FQ], "bfloat16"),
     "pd": ("dram", [4 * Q, 128, FQ], "bfloat16"),
-    "wd": ("dram", [2, 128, M], "bfloat16"),
+    "wd": ("dram", [2 * Q, 128, MQ], "bfloat16"),
     "z": ("sbuf", [128, 4 * F], "bfloat16"),
     "ww": ("sbuf", [128, 2 * M], "bfloat16"),
     "tb": ("sbuf", [128, 2 * F], "bfloat16"),
@@ -19,7 +21,7 @@ SCRATCH = {
     "ysb": ("sbuf", [128, F], "bfloat16"),
     "yp": ("psum", [128, 512], "float32"),
 }
-SEMAPHORES = ["ld", "lw", "hx", "w0", "w1", "p", "s", "lz", "lww", "v", "mm", "cp", "st"]
+SEMAPHORES = ["ld", "lw", "hx", "sc", "w0", "w1", "p", "pf", "s", "lz", "lww", "v", "mm", "cp", "st"]
 
 
 def _plan(cores, groups, topo):
@@ -37,31 +39,33 @@ def _plan(cores, groups, topo):
     def ok(a, b):
         return topo.may_write(cores[a], cores[b])
 
-    def off(a, b):
-        return topo.chip(cores[a]) != topo.chip(cores[b])
-
     xdst = [[[d for d in mem[rk[r]] if pos[d] == k and d != r] for k in range(Q)] for r in range(n)]
     pdst = [[d for d in range(n) if d != r and ((rk[d] == rk[r] and (hs[d] == hs[r] or pos[d] == pos[r]))
                                                 or (rk[d] != rk[r] and ok(r, d)))] for r in range(n)]
-    duty = [0] * n
-    w1, w2 = [], []
+    sca, gat = [], []
     for o in lead:
-        near = [r for r in mem[rk[o]] if hs[r] != hs[o]]
-        far = [r for r in range(n) if rk[r] != rk[o] and ok(o, r)]
-        diag = [r for r in range(n) if rk[r] != rk[o] and not ok(o, r)]
-        b = min(far, key=lambda r: (duty[r], off(r, o), r))
-        a = sorted(near, key=lambda r: (duty[r], off(r, o), r))[:2]
-        for r in a + [b]:
-            duty[r] += 1
-        out = {o: [r for r in hm[hs[o]] if r != o], b: [r for r in far if r != b]}
-        for r in a:
-            out[r] = []
-        for d in [r for r in near if r not in a] + diag:
-            s = min([s for s in a if ok(s, d)], key=lambda s: (len(out[s]), off(s, d), s))
-            out[s].append(d)
-        w1.append(a + [b])
-        w2.append(out)
-    return lead, rk, mem, pos, xdst, pdst, w1, w2
+        h0 = hs[o]
+        h1 = [h for h in hm if h != h0 and topo.rack(h) == rk[o]][0]
+        h3 = [h for h in hm if topo.rack(h) != rk[o] and ok(o, hm[h][0])][0]
+        h2 = [h for h in hm if topo.rack(h) != rk[o] and not ok(o, hm[h][0])][0]
+        sc, ga = [], {}
+        for qq in range(Q):
+            ha, hb, hc = hm[h0][qq], hm[h1][qq], hm[h3][qq]
+            to = [r for r in (ha, hb, hc) if r != o]
+            rest0 = [r for r in hm[h0] if r not in (o, ha)]
+            if ha == o:
+                to.append(rest0[0])
+                rest0 = rest0[1:]
+            r1 = [hm[h1][(qq + i) % Q] for i in range(1, Q)]
+            r3 = [hm[h3][(qq + i) % Q] for i in range(1, Q)]
+            r2 = [hm[h2][(qq + i) % Q] for i in range(Q)]
+            sc.append(to)
+            ga[ha] = (qq, rest0 + r1[:1] + r3[:1])
+            ga[hb] = (qq, r2[:2] + r1[1:])
+            ga[hc] = (qq, r2[2:] + r3[1:])
+        sca.append(sc)
+        gat.append(ga)
+    return lead, rk, mem, pos, xdst, pdst, sca, gat
 
 
 def _bits(topo, src, dests):
@@ -89,7 +93,7 @@ def rank_program(g, core, T, topo):
         return
     cores, groups = T.cores, T.tables["GROUPS"]
     n = len(cores)
-    lead, rk, mem, pos, xdst, pdst, w1, w2 = _plan(cores, groups, topo)
+    lead, rk, mem, pos, xdst, pdst, sca, gat = _plan(cores, groups, topo)
     sem, v, te = T.sem, g.vector, g.tensor
     wsem = [sem.w0, sem.w1]
     q = rk[rank]
@@ -101,74 +105,59 @@ def rank_program(g, core, T, topo):
     def cs(ranks):
         return [cores[r] for r in ranks]
 
-    def xbits(r):
-        return _bits(topo, cores[r], cs([d for d in mem[rk[r]] if d != r]))
-
-    def pbits(r):
-        return _bits(topo, cores[r], cs(pdst[r]))
-
-    def send_w(gi, to):
-        b = _bits(topo, core, cs(to))
-        g.remote_dma_fused([RemoteDMATransfer(dst_ids=_ids(topo, core, cs(to)), dma_engine_mask=_m(b), remote_sem=wsem[gi],
-                                              srcs=[T.wd[gi]], dsts=[T.wd[gi] for _ in to])], local_sem=sem.s)
-        sent[0] += len(b)
+    def call(parts):
+        b = _bits(topo, core, cs([d for _, _, to in parts for d, _ in to]))
+        assert len(parts) * EP <= len(b)
+        trs = [RemoteDMATransfer(dst_ids=_ids(topo, core, cs([d for d, _ in to])), dma_engine_mask=_m(b[i * EP:(i + 1) * EP]),
+                                 remote_sem=rsem, srcs=srcs, alu_op=(1 if len(srcs) > 1 else 0), dsts=[ap for _, ap in to])
+               for i, (rsem, srcs, to) in enumerate(parts)]
+        g.remote_dma_fused(trs, local_sem=sem.s)
+        sent[0] += len(parts) * EP
 
     g.sync.dma_start(T.xq[:], T.x[:, :]).then_inc(sem.ld, 16)
     for gi in own:
-        g.scalar.dma_start(T.wd[gi], T.w[:, :]).then_inc(sem.lw, 16)
+        g.scalar.dma_start(T.wd[gi * Q:(gi + 1) * Q], T.w[:, :]).then_inc(sem.lw, 16)
 
-    b = xbits(rank)
-    e = len(b) // Q
-    trs = []
-    for j in range(Q):
-        to = cs(xdst[rank][j])
-        trs.append(RemoteDMATransfer(dst_ids=_ids(topo, core, to), dma_engine_mask=_m(b[j * e:(j + 1) * e]), remote_sem=sem.hx,
-                                     srcs=[T.xq[j]], dsts=[T.xs[mine.index(rank)] for _ in to]))
-        sent[0] += e
     g.wait_ge(sem.ld, 16)
-    g.remote_dma_fused(trs, local_sem=sem.s)
+    call([(sem.hx, [T.xq[j]], [(d, T.xs[mine.index(rank)]) for d in xdst[rank][j]]) for j in range(Q)])
 
     for gi in own:
         g.wait_ge(sem.lw, 16 * len(own))
-        send_w(gi, w1[gi])
+        call([(sem.sc, [T.wd[gi * Q + j]], [(d, T.wd[gi * Q + j]) for d in sca[gi][j]]) for j in range(Q)])
 
-    g.wait_ge(sem.hx, sum(len(xbits(o)) // Q for o in mine if o != rank))
-    b = pbits(rank)
-    h = len(b) // 2
-    trs = []
+    g.wait_ge(sem.hx, EP * (len(mine) - 1))
+    parts = []
     for gi in range(2):
         srcs = [(T.xq[k] if r == rank else T.xs[mine.index(r)]) for r in groups[gi] if r in mine]
         assert srcs
-        trs.append(RemoteDMATransfer(dst_ids=_ids(topo, core, cs(pdst[rank])), dma_engine_mask=_m(b[gi * h:(gi + 1) * h]),
-                                     remote_sem=sem.p, srcs=srcs, alu_op=(1 if len(srcs) > 1 else 0),
-                                     dsts=[T.pd[(0 if rk[d] == q else 2 * Q) + gi * Q + k] for d in pdst[rank]]))
-        sent[0] += h
-    g.remote_dma_fused(trs, local_sem=sem.s)
+        parts.append((sem.p, srcs, [(d, T.pd[gi * Q + k]) for d in pdst[rank] if rk[d] == q]))
+        parts.append((sem.pf, srcs, [(d, T.pd[2 * Q + gi * Q + k]) for d in pdst[rank] if rk[d] != q]))
+    call(parts)
 
-    def w_in(gi):
-        for s in [lead[gi]] + list(w2[gi]):
-            to = w1[gi] if (s == lead[gi] and rank in w1[gi]) else w2[gi][s]
-            if rank in to:
-                return len(_bits(topo, cores[s], cs(to)))
-        return 0
-
-    for gi in own:
-        send_w(gi, w2[gi][rank])
+    sc_in = sum(EP for gi in range(2) for to in sca[gi] if rank in to)
+    if sc_in:
+        g.wait_ge(sem.sc, sc_in)
+    parts = []
     for gi in range(2):
-        if gi not in own and rank in w2[gi] and w2[gi][rank]:
-            g.wait_ge(wsem[gi], w_in(gi))
-            send_w(gi, w2[gi][rank])
+        if rank in gat[gi]:
+            j, to = gat[gi][rank]
+            hf = (len(to) + 1) // 2
+            for sh in (to[:hf], to[hf:]):
+                parts.append((wsem[gi], [T.wd[gi * Q + j]], [(d, T.wd[gi * Q + j]) for d in sh]))
+    if parts:
+        call(parts)
 
-    npd = sum(2 * (len(pbits(s)) // 2) for s in range(n) if rank in pdst[s])
     for i, qu in enumerate((g.sync, g.scalar)):
-        qu.wait_ge(sem.p, npd)
+        qu.wait_ge((sem.p, sem.pf)[i], sum(2 * EP for s in range(n) if rank in pdst[s] and (rk[s] != q) == bool(i)))
         qu.dma_start(T.z[:, i * 2 * F:(i + 1) * 2 * F], T.pd[i * 2 * Q:(i + 1) * 2 * Q]).then_inc(sem.lz, 16)
     for gi, qu in enumerate((g.sync, g.scalar)):
         if gi in own:
             qu.wait_ge(sem.lw, 16 * len(own))
         else:
-            qu.wait_ge(wsem[gi], w_in(gi))
-        qu.dma_start(T.ww[gi * 64:(gi + 1) * 64, :], T.wd[gi]).then_inc(sem.lww, 16)
+            if sc_in:
+                qu.wait_ge(sem.sc, sc_in)
+            qu.wait_ge(wsem[gi], sum(EP for s in gat[gi] if rank in gat[gi][s][1]))
+        qu.dma_start(T.ww[gi * 64:(gi + 1) * 64, :], T.wd[gi * Q:(gi + 1) * Q]).then_inc(sem.lww, 16)
 
     v.wait_ge(sem.lz, 32)
     v.tensor_tensor(out=T.tb[:, :], in0=T.z[:, 0:2 * F], in1=T.z[:, 2 * F:4 * F], op=AluOpType.add).then_inc(sem.v, 1)

from concourse.bass import DstId, RemoteDMATransfer
from concourse.mybir import AluOpType

F = 64
M = 128
HALF = 8
Q = 4
FQ = F // Q
MQ = M // Q
EP = 2

SCRATCH = {
    "xq": ("dram", [Q, 128, FQ], "bfloat16"),
    "xs": ("dram", [HALF, 128, FQ], "bfloat16"),
    "pd": ("dram", [4 * Q, 128, FQ], "bfloat16"),
    "wd": ("dram", [2 * Q, 128, MQ], "bfloat16"),
    "z": ("sbuf", [128, 4 * F], "bfloat16"),
    "ww": ("sbuf", [128, 2 * M], "bfloat16"),
    "tb": ("sbuf", [128, 2 * F], "bfloat16"),
    "t": ("sbuf", [128, 2 * F], "bfloat16"),
    "ysb": ("sbuf", [128, F], "bfloat16"),
    "yp": ("psum", [128, 512], "float32"),
}
SEMAPHORES = ["ld", "lw", "hx", "sc", "w0", "w1", "p", "pf", "s", "lz", "lww", "v", "mm", "cp", "st"]


def _plan(cores, groups, topo):
    n = len(cores)
    lead = [mem[0] for mem in groups]
    hs = [topo.host(c) for c in cores]
    rk = [topo.rack(h) for h in hs]
    hm, mem = {}, {}
    for r in sorted(range(n), key=lambda r: topo.chip(cores[r])):
        hm.setdefault(hs[r], []).append(r)
    for r in range(n):
        mem.setdefault(rk[r], []).append(r)
    pos = [hm[hs[r]].index(r) for r in range(n)]

    def ok(a, b):
        return topo.may_write(cores[a], cores[b])

    xdst = [[[d for d in mem[rk[r]] if pos[d] == k and d != r] for k in range(Q)] for r in range(n)]
    pdst = [[d for d in range(n) if d != r and ((rk[d] == rk[r] and (hs[d] == hs[r] or pos[d] == pos[r]))
                                                or (rk[d] != rk[r] and ok(r, d)))] for r in range(n)]
    sca, gat = [], []
    for o in lead:
        h0 = hs[o]
        h1 = [h for h in hm if h != h0 and topo.rack(h) == rk[o]][0]
        h3 = [h for h in hm if topo.rack(h) != rk[o] and ok(o, hm[h][0])][0]
        h2 = [h for h in hm if topo.rack(h) != rk[o] and not ok(o, hm[h][0])][0]
        sc, ga = [], {}
        for qq in range(Q):
            ha, hb, hc = hm[h0][qq], hm[h1][qq], hm[h3][qq]
            to = [r for r in (ha, hb, hc) if r != o]
            rest0 = [r for r in hm[h0] if r not in (o, ha)]
            if ha == o:
                to.append(rest0[0])
                rest0 = rest0[1:]
            r1 = [hm[h1][(qq + i) % Q] for i in range(1, Q)]
            r3 = [hm[h3][(qq + i) % Q] for i in range(1, Q)]
            r2 = [hm[h2][(qq + i) % Q] for i in range(Q)]
            sc.append(to)
            ga[ha] = (qq, rest0 + r1[:1] + r3[:1])
            ga[hb] = (qq, r2[:2] + r1[1:])
            ga[hc] = (qq, r2[2:] + r3[1:])
        sca.append(sc)
        gat.append(ga)
    return lead, rk, mem, pos, xdst, pdst, sca, gat


def _bits(topo, src, dests):
    m = topo.mask(src, dests[0])
    for d in dests[1:]:
        m &= topo.mask(src, d)
    return [i for i in range(16) if (m >> i) & 1]


def _m(bits):
    return sum(1 << i for i in bits)


def _ids(topo, core, dests):
    out = []
    for d in dests:
        rid, pid = topo.addr(d, core)
        out.append(DstId(rid=rid, pnc=pid))
    return out


def rank_program(g, core, T, topo):
    rank = T.rank_of(core)
    if rank is None:
        return
    cores, groups = T.cores, T.tables["GROUPS"]
    n = len(cores)
    lead, rk, mem, pos, xdst, pdst, sca, gat = _plan(cores, groups, topo)
    sem, v, te = T.sem, g.vector, g.tensor
    wsem = [sem.w0, sem.w1]
    q = rk[rank]
    mine = mem[q]
    k = pos[rank]
    own = [gi for gi in range(2) if lead[gi] == rank]
    sent = [0]

    def cs(ranks):
        return [cores[r] for r in ranks]

    def call(parts):
        b = _bits(topo, core, cs([d for _, _, to in parts for d, _ in to]))
        assert len(parts) * EP <= len(b)
        trs = [RemoteDMATransfer(dst_ids=_ids(topo, core, cs([d for d, _ in to])), dma_engine_mask=_m(b[i * EP:(i + 1) * EP]),
                                 remote_sem=rsem, srcs=srcs, alu_op=(1 if len(srcs) > 1 else 0), dsts=[ap for _, ap in to])
               for i, (rsem, srcs, to) in enumerate(parts)]
        g.remote_dma_fused(trs, local_sem=sem.s)
        sent[0] += len(parts) * EP

    g.sync.dma_start(T.xq[:], T.x[:, :]).then_inc(sem.ld, 16)
    for gi in own:
        g.scalar.dma_start(T.wd[gi * Q:(gi + 1) * Q], T.w[:, :]).then_inc(sem.lw, 16)

    g.wait_ge(sem.ld, 16)
    call([(sem.hx, [T.xq[j]], [(d, T.xs[mine.index(rank)]) for d in xdst[rank][j]]) for j in range(Q)])

    for gi in own:
        g.wait_ge(sem.lw, 16 * len(own))
        call([(sem.sc, [T.wd[gi * Q + j]], [(d, T.wd[gi * Q + j]) for d in sca[gi][j]]) for j in range(Q)])

    g.wait_ge(sem.hx, EP * (len(mine) - 1))
    parts = []
    for gi in range(2):
        srcs = [(T.xq[k] if r == rank else T.xs[mine.index(r)]) for r in groups[gi] if r in mine]
        assert srcs
        parts.append((sem.p, srcs, [(d, T.pd[gi * Q + k]) for d in pdst[rank] if rk[d] == q]))
        parts.append((sem.pf, srcs, [(d, T.pd[2 * Q + gi * Q + k]) for d in pdst[rank] if rk[d] != q]))
    call(parts)

    sc_in = sum(EP for gi in range(2) for to in sca[gi] if rank in to)
    if sc_in:
        g.wait_ge(sem.sc, sc_in)
    parts = []
    for gi in range(2):
        if rank in gat[gi]:
            j, to = gat[gi][rank]
            hf = (len(to) + 1) // 2
            for sh in (to[:hf], to[hf:]):
                parts.append((wsem[gi], [T.wd[gi * Q + j]], [(d, T.wd[gi * Q + j]) for d in sh]))
    if parts:
        call(parts)

    for i, qu in enumerate((g.sync, g.scalar)):
        qu.wait_ge((sem.p, sem.pf)[i], sum(2 * EP for s in range(n) if rank in pdst[s] and (rk[s] != q) == bool(i)))
        qu.dma_start(T.z[:, i * 2 * F:(i + 1) * 2 * F], T.pd[i * 2 * Q:(i + 1) * 2 * Q]).then_inc(sem.lz, 16)
    for gi, qu in enumerate((g.sync, g.scalar)):
        if gi in own:
            qu.wait_ge(sem.lw, 16 * len(own))
        else:
            if sc_in:
                qu.wait_ge(sem.sc, sc_in)
            qu.wait_ge(wsem[gi], sum(EP for s in gat[gi] if rank in gat[gi][s][1]))
        qu.dma_start(T.ww[gi * 64:(gi + 1) * 64, :], T.wd[gi * Q:(gi + 1) * Q]).then_inc(sem.lww, 16)

    v.wait_ge(sem.lz, 32)
    v.tensor_tensor(out=T.tb[:, :], in0=T.z[:, 0:2 * F], in1=T.z[:, 2 * F:4 * F], op=AluOpType.add).then_inc(sem.v, 1)
    v.wait_ge(sem.v, 1)
    v.tensor_scalar(out=T.t[:, :], in0=T.tb[:, :], scalar1=0.0, scalar2=None, op0=AluOpType.max).then_inc(sem.v, 1)

    te.wait_ge(sem.lww, 32)
    te.wait_ge(sem.v, 2)
    te.matmul(T.yp[:, 0:F], T.ww[:, 0:M], T.t[:, 0:F], True, False)
    te.matmul(T.yp[:, 0:F], T.ww[:, M:2 * M], T.t[:, F:2 * F], False, True).then_inc(sem.mm, 1)
    v.wait_ge(sem.mm, 1)
    v.tensor_copy(T.ysb[:, :], T.yp[:, 0:F]).then_inc(sem.cp, 1)
    g.sync.wait_ge(sem.cp, 1)
    g.sync.dma_start(T.y[:, :], T.ysb[:, :]).then_inc(sem.st, 16)

    g.wait_ge(sem.s, sent[0])
    g.wait_ge(sem.st, 16)
